import numpy as np
import ml_dtypes


def mxq(x, axis, fmt="e4m3"):
    dtype, down = {"e4m3": (ml_dtypes.float8_e4m3fn, 7), "e5m2": (ml_dtypes.float8_e5m2, 14)}[fmt]
    v = np.moveaxis(np.asarray(x, np.float32).astype(ml_dtypes.bfloat16).astype(np.float64), axis, -1)
    blocks = v.reshape(v.shape[:-1] + (-1, 32))
    amax = np.abs(blocks).max(-1, keepdims=True)
    byte = np.maximum(np.where(amax > 0, np.frexp(amax)[1] - 1 + 127, 0) - down, 1)
    scale = np.exp2(byte - 127.0)
    codes = (blocks / scale).astype(np.float32).astype(dtype).astype(np.float64)
    return np.moveaxis((codes * scale).reshape(v.shape), -1, axis)


WIDE = False


def mx_kscale(k):
    if not WIDE:
        return np.ones(k)
    levels = np.array([10, -10, 5, -5, 0])
    if k % 512:
        return np.exp2(np.random.permutation(np.resize(levels, k // 32))).repeat(32)
    a = np.empty((k // 512, 16))
    for p in range(k // 512):
        a[p, :8] = np.random.permutation(np.resize(levels, 8))
        for g in range(8):
            far = levels[np.abs(levels - a[p, g]) >= 10]
            a[p, g + 8] = far[np.random.randint(len(far))]
    return np.exp2(a.ravel()).repeat(32)


def f64(x):
    return np.asarray(x).astype(np.float64)


def striped(idx):
    return np.tile(idx.reshape(-1, 16).T, (8, 1)).astype(np.uint16)


def unstriped(offs):
    return offs[:16].T.reshape(-1).astype(np.int64)


def striped8(idx):
    return np.concatenate([x.reshape(-1, 16).T for x in idx]).astype(np.uint16)


def runs(offs, k):
    lists = np.stack([offs[16 * r : 16 * r + 16].T.reshape(-1) for r in range(8)]).astype(np.int64)
    return lists[np.arange(k) % 512 // 64]


def pack_weight(w):
    k, n = w.shape
    w = f64(np.asarray(w, np.float32).astype(ml_dtypes.bfloat16)).reshape(k // 32, 32, n)
    amax = np.abs(w).max(1)
    byte = np.clip(np.where(amax > 0, np.frexp(amax)[1] - 1 + 127 - 7, 1), 1, 254)
    scaled = (w * np.exp2(127.0 - byte)[:, None, :]).reshape(k, n).astype(np.float32)
    words = np.ascontiguousarray(scaled.reshape(k // 512, 128, 4, n).transpose(0, 1, 3, 2)).astype(ml_dtypes.float8_e4m3fn).view(np.uint8)
    return words, np.ascontiguousarray(byte.astype(np.uint8).reshape(k // 512, 16, n))


def unpack_weight(words, scales):
    g, p, n, _ = words.shape
    vals = np.ascontiguousarray(words).view(ml_dtypes.float8_e4m3fn).astype(np.float64) * np.repeat(np.exp2(scales.astype(np.float64) - 127.0), 8, axis=1)[..., None]
    return vals.transpose(0, 1, 3, 2).reshape(g * 512, n)


def sigmoid(v):
    return 1.0 / (1.0 + np.exp(-np.maximum(v, -700.0)))


K, T, S, V, H = 512, 2048, 512, 512, 512


def setup_inputs():
    n = np.random.standard_normal
    s = mx_kscale(K)[:, None]
    u = mx_kscale(S)
    packed_xT = pack_weight(n((K, T)) * s)
    return {
        "x_words": packed_xT[0],
        "x_scales": packed_xT[1],
        "w1": (n((K, H)) / np.sqrt(K) / s).astype(np.float32),
        "w2": (n((K, H)) / np.sqrt(K) / s).astype(np.float32),
        "w3": (n((K, H)) / np.sqrt(K) / s).astype(np.float32),
        "ga": (np.random.uniform(0.5, 1.5, (H, 1)) * u[:, None]).astype(np.float32),
        "gb": (np.random.uniform(0.5, 1.5, (H, 1)) / u[:, None]).astype(np.float32),
        "offs": striped(np.random.permutation(T)[:S]),
        "two": striped(np.random.permutation(T)[:S]),
        "n1": striped8(np.stack([np.random.permutation(S) for _ in range(8)])),
        "n2": striped8(np.stack([np.random.permutation(S) for _ in range(8)])),
        "n3": striped8(np.stack([np.random.permutation(S) for _ in range(8)])),
        "three": striped(np.random.permutation(T)[:V]),
        "n4": striped8(np.stack([np.random.permutation(V) for _ in range(8)])),
        "n5": striped8(np.stack([np.random.permutation(V) for _ in range(8)])),
        "n6": striped8(np.stack([np.random.permutation(V) for _ in range(8)])),
        "n7": striped8(np.stack([np.random.permutation(V) for _ in range(8)])),
    }


def reference(x_words, x_scales, w1, w2, w3, ga, gb, offs, two, n1, n2, n3, three, n4, n5, n6, n7):
    x_two = unpack_weight(x_words, x_scales)[:, unstriped(two)]
    d = mxq(f64(w2), 0, "e4m3").T @ x_two
    xq = unpack_weight(x_words, x_scales)[:, unstriped(offs)]
    y = mxq(f64(w1), 0, "e4m3").T @ xq
    z = f64(ga) * (d * (y[np.arange(H)[:, None], runs(n1, H)] - y) + 0.5 * ((d[np.arange(H)[:, None], runs(n3, H)]) * (y[np.arange(H)[:, None], runs(n2, H)] - y)))
    x_three = unpack_weight(x_words, x_scales)[:, unstriped(three)]
    b = mxq(f64(w3), 0, "e4m3").T @ x_three
    b1 = b[np.arange(H)[:, None], runs(n4, H)]
    b2 = b[np.arange(H)[:, None], runs(n5, H)]
    b3 = b[np.arange(H)[:, None], runs(n6, H)]
    z2 = f64(gb) * (np.maximum(np.maximum(b1, b2), b3) - (0.5 * (np.maximum(np.minimum(b1, b2), np.minimum(np.maximum(b1, b2), b3)))))
    s = 0.0625 * ((mxq(z, 0, "e4m3").T @ mxq(z2, 0, "e4m3")))
    st = s * (sigmoid(s[np.arange(S)[:, None], runs(n7, S)]))
    return np.maximum(st, st[np.arange(S)[:, None], runs(n7, S)])

@@ -1,0 +1,230 @@
+from contextlib import ExitStack
+
+import concourse.mybir as mybir
+
+K, T, S, H = 512, 2048, 512, 512
+FLOPS = 4 * 2 * 512 * 512 * 512
+
+F32 = mybir.dt.float32
+BF16 = mybir.dt.bfloat16
+I32 = mybir.dt.int32
+U32 = mybir.dt.uint32
+U16 = mybir.dt.uint16
+U8 = mybir.dt.uint8
+FP8X4 = mybir.dt.float8_e4m3fn_x4
+ALU = mybir.AluOpType
+ACT = mybir.ActivationFunctionType
+
+P = 128
+PACK = 4
+WIN = 2 * S
+
+
+def tile_picked_twkflowbtop2twicp_none_p_kernel(
+    tc, x_words, x_scales, w1, w2, w3, ga, gb, offs, two, n1, n2, n3, three, n4, n5, n6, n7, out
+):
+    nc = tc.nc
+    with ExitStack() as ctx:
+        keep = ctx.enter_context(tc.tile_pool(name="keep", bufs=1))
+        work = ctx.enter_context(tc.tile_pool(name="work", bufs=2))
+        psum = ctx.enter_context(tc.psum_pool(name="psum", bufs=1))
+
+        def load_list(name, src):
+            tile = keep.tile([P, S // 16], U16, name=name)
+            nc.sync.dma_start(tile[:], src)
+            return tile
+
+        def load_weight(name, src):
+            raw = keep.tile([P, PACK, H], F32, name=name)
+            nc.sync.dma_start(raw[:], src.rearrange("(p j) c -> p j c", j=PACK))
+            return raw
+
+        table_bytes = keep.tile([P, T], U8, name="table_bytes", align_bytes=64)
+        l_three = load_list("l_three", three)
+        l_offs = load_list("l_offs", offs)
+        l_two = load_list("l_two", two)
+        for q in range(4):
+            nc.sync.dma_start(
+                table_bytes[32 * q : 32 * (q + 1), :].bitcast(I32),
+                x_scales[0, 4 * q : 4 * q + 4, :].bitcast(I32).unsqueeze(0).broadcast_to([8, 4, T // 4]),
+            )
+        raw3 = load_weight("raw3", w3)
+        table_words = keep.tile([P, T], U32, name="table_words", align_bytes=64)
+        nc.sync.dma_start(table_words[:].bitcast(I32), x_words[0].rearrange("p n t -> p (n t)").bitcast(I32))
+        l4 = load_list("l4", n4)
+        l5 = load_list("l5", n5)
+        l6 = load_list("l6", n6)
+        raw1 = load_weight("raw1", w1)
+        raw2 = load_weight("raw2", w2)
+        l1 = load_list("l1", n1)
+        l2 = load_list("l2", n2)
+        l3 = load_list("l3", n3)
+        l7 = load_list("l7", n7)
+
+        ga_t = keep.tile([P, PACK], F32, name="ga_t")
+        gb_t = keep.tile([P, PACK], F32, name="gb_t")
+        nc.gpsimd.dma_start(gb_t[:], gb.rearrange("(p t) o -> p (t o)", t=PACK))
+        nc.gpsimd.dma_start(ga_t[:], ga.rearrange("(p t) o -> p (t o)", t=PACK))
+        half_sign = keep.tile([P, PACK], F32, name="half_sign")
+        gah = keep.tile([P, PACK], F32, name="gah")
+        gbh = keep.tile([P, PACK], F32, name="gbh")
+        nc.gpsimd.tensor_scalar(half_sign[:], gb_t[:], 0.0, -0.5, ALU.is_ge, ALU.add)
+        nc.gpsimd.tensor_tensor(gbh[:], gb_t[:], half_sign[:], ALU.mult)
+        nc.gpsimd.tensor_tensor(gah[:], ga_t[:], half_sign[:], ALU.mult)
+
+        def pick_bytes(name, lst):
+            got = keep.tile([P, S], U8, name=name, align_bytes=64)
+            nc.vector.tensor_copy(got[:], table_bytes[:].indirect(lst[:]))
+            return got
+
+        def pick_words(name, lst):
+            got = keep.tile([P, S], U32, name=name, align_bytes=64)
+            nc.vector.tensor_copy(got[:], table_words[:].indirect(lst[:]))
+            return got
+
+        def cast_weight(name, raw):
+            grouped = keep.tile([P, PACK * H], BF16, name=name, align_bytes=64)
+            nc.scalar.copy(
+                grouped[:].rearrange("p (t m j) -> p m j t", t=PACK, j=PACK),
+                raw[:].rearrange("p j (m t) -> p m j t", t=PACK),
+            )
+            return grouped
+
+        def quantize(name, grouped, width):
+            codes = keep.tile([P, width], U32, name=name + "_c", align_bytes=64)
+            scales = keep.tile([P, width], U8, name=name + "_s", align_bytes=64)
+            nc.vector.quantize_mx(out=codes[:].bitcast(FP8X4), scales=scales[:], in_=grouped)
+            return codes, scales
+
+        def product(bank, lhs, lhs_cols, rhs):
+            acc = psum.tile([P, S], F32, name="bank%d" % bank)
+            nc.tensor.matmul_mx(
+                out=acc[:],
+                lhsT=lhs[0][:, lhs_cols].bitcast(FP8X4),
+                lhsT_scale=lhs[1][:, lhs_cols],
+                rhs=rhs[0][:].bitcast(FP8X4),
+                rhs_scale=rhs[1][:],
+                start=True,
+                stop=True,
+            )
+            return acc
+
+        def window(name):
+            return keep.tile([P, WIN], F32, name=name)
+
+        def fetch(engine, dst, win, lst):
+            if engine == "S":
+                nc.scalar.activation(dst, win[:].indirect(lst), ACT.Copy)
+            else:
+                nc.vector.tensor_copy(dst, win[:].indirect(lst))
+
+        tiles = range(PACK)
+        by3 = pick_bytes("by3", l_three)
+        g3 = cast_weight("g3", raw3)
+        by1 = pick_bytes("by1", l_offs)
+        by2 = pick_bytes("by2", l_two)
+        q3 = quantize("q3", g3[:], H)
+        wd3 = pick_words("wd3", l_three)
+        b_ps = [product(t, q3, slice(P * t, P * (t + 1)), (wd3, by3)) for t in tiles]
+        b_win = [window("b_win%d" % t) for t in tiles]
+        wd1 = pick_words("wd1", l_offs)
+        wd2 = pick_words("wd2", l_two)
+
+        z2b = keep.tile([P, PACK, S], BF16, name="z2b", align_bytes=64)
+        zb = keep.tile([P, PACK, S], BF16, name="zb", align_bytes=64)
+        B_ENG = ["VVV","SSS","SSS","SSS"]
+
+        def b_tile(t):
+            if t in (0,):
+                nc.vector.tensor_scalar(b_win[t][:, 0:S], b_ps[t][:], gbh[:, t : t + 1], None, ALU.mult)
+            else:
+                nc.scalar.activation(b_win[t][:, 0:S], b_ps[t][:], ACT.Copy, scale=gbh[:, t : t + 1])
+            got = [work.tile([P, S], F32, name="bg%d" % i, bufs=4) for i in range(3)]
+            for g, lst, eng in zip(got, (l4, l5, l6), B_ENG[t]):
+                fetch(eng, g[:], b_win[t], lst[:])
+            hi = work.tile([P, S], F32, name="hi")
+            lo = work.tile([P, S], F32, name="lo")
+            mid = work.tile([P, S], F32, name="mid")
+            nc.vector.tensor_tensor(hi[:], got[0][:], got[1][:], ALU.max)
+            nc.vector.tensor_tensor(lo[:], got[0][:], got[1][:], ALU.min)
+            nc.vector.tensor_tensor(mid[:], hi[:], got[2][:], ALU.min)
+            nc.vector.tensor_tensor(hi[:], hi[:], got[2][:], ALU.max)
+            nc.vector.tensor_tensor(mid[:], lo[:], mid[:], ALU.max)
+            nc.vector.scalar_tensor_tensor(z2b[:, t, :], hi[:], 2.0, mid[:], ALU.mult, ALU.subtract)
+
+        y_win = [window("y_win%d" % t) for t in tiles]
+        d_win = [window("d_win%d" % t) for t in tiles]
+
+        def y_tile(t):
+            nc.scalar.copy(y_win[t][:, 0:S], y_ps[t][:])
+            y1 = work.tile([P, S], F32, name="y1", bufs=4)
+            y2 = work.tile([P, S], F32, name="y2", bufs=4)
+            fetch("S", y2[:], y_win[t], l2[:])
+            nc.scalar.activation(d_win[t][:, 0:S], d_ps[t][:], ACT.Copy, scale=gah[:, t : t + 1])
+            fetch("S", y1[:], y_win[t], l1[:])
+            p2 = work.tile([P, S], F32, name="p2", bufs=4)
+            nc.vector.tensor_tensor(y2[:], y2[:], y_win[t][:, 0:S], ALU.subtract)
+            if t in (0, 1):
+                nc.vector.tensor_tensor(p2[:], d_win[t][:].indirect(l3[:]), y2[:], ALU.mult)
+            else:
+                fetch("S", p2[:], d_win[t], l3[:])
+                nc.vector.tensor_tensor(p2[:], p2[:], y2[:], ALU.mult)
+            nc.vector.tensor_tensor(y1[:], y1[:], y_win[t][:, 0:S], ALU.subtract)
+            nc.vector.scalar_tensor_tensor(y1[:], d_win[t][:, 0:S], 2.0, y1[:], ALU.mult, ALU.mult)
+            nc.vector.tensor_tensor(zb[:, t, :], y1[:], p2[:], ALU.add)
+
+        g1 = cast_weight("g1", raw1)
+        g2 = cast_weight("g2", raw2)
+        b_tile(0)
+        q1 = quantize("q1", g1[:], H)
+        y_ps = [product(4 + t, q1, slice(P * t, P * (t + 1)), (wd1, by1)) for t in tiles]
+        q2 = quantize("q2", g2[:], H)
+        b_tile(1)
+        b_tile(2)
+        b_tile(3)
+        d_ps = [product(t, q2, slice(P * t, P * (t + 1)), (wd2, by2)) for t in tiles]
+        for t in tiles:
+            y_tile(t)
+
+        z2g = keep.tile([P, PACK * S], BF16, name="z2g", align_bytes=64)
+        mov_c = keep.tile([P, S], U32, name="mov_c", align_bytes=64)
+        mov_s = keep.tile([P, S], U8, name="mov_s", align_bytes=64)
+        half = S // 2
+        for h in range(2):
+            piece = z2g[:, PACK * half * h : PACK * half * (h + 1)]
+            weave = nc.scalar.copy if "SS"[h] == "S" else nc.vector.tensor_copy
+            weave(
+                piece.rearrange("p (c i t) -> p c t i", t=PACK, i=4),
+                z2b[:, :, half * h : half * (h + 1)].rearrange("p t (c i) -> p c t i", i=4),
+            )
+            cols = slice(half * h, half * (h + 1))
+            nc.vector.quantize_mx(out=mov_c[:, cols].bitcast(FP8X4), scales=mov_s[:, cols], in_=piece)
+
+        out_rows = out.rearrange("(g u q) v -> u g q v", u=PACK, q=8)
+        s_win = b_win
+        st_win = d_win
+        for u in tiles:
+            zg = keep.tile([P, PACK * P], BF16, name="zg%d" % u, align_bytes=64)
+            nc.vector.tensor_copy(
+                zg[:].rearrange("p (g h i t) -> p g h t i", h=2, i=4, t=PACK),
+                zb[:].rearrange("p t (g u h i) -> p u g h t i", u=PACK, h=2, i=4)[:, u],
+            )
+            qz = quantize("qz%d" % u, zg[:], P)
+            s_ps = product(4 + u, qz, slice(0, P), (mov_c, mov_s))
+            if u in (0, 1, 2, 3):
+                nc.vector.tensor_scalar(s_win[u][:, 0:S], s_ps[:], 0.0625, None, ALU.mult)
+            else:
+                nc.scalar.mul(s_win[u][:, 0:S], s_ps[:], 0.0625)
+        for u in tiles:
+            gate = work.tile([P, S], F32, name="gate", bufs=4)
+            nc.scalar.activation(gate[:], s_win[u][:].indirect(l7[:]), ACT.Sigmoid)
+            nc.vector.tensor_tensor(st_win[u][:, 0:S], s_win[u][:, 0:S], gate[:], ALU.mult)
+        for u in tiles:
+            other = work.tile([P, S], F32, name="other", bufs=4)
+            engs = ["V","S","S","SS"][u]
+            n = S // len(engs)
+            for k, eng in enumerate(engs):
+                cols = slice(n * k, n * (k + 1))
+                fetch(eng, other[:, cols], st_win[u], l7[:, n // 16 * k : n // 16 * (k + 1)])
+                nc.vector.tensor_tensor(other[:, cols], st_win[u][:, cols], other[:, cols], ALU.max)
+                nc.sync.dma_start(out_rows[u][:, :, cols], other[:, cols])

@@ -35,42 +35,35 @@ def tile_picked_twkflowbtop2twicp_none_p_kernel(
             return tile
 
         def load_weight(name, src):
-            raw = keep.tile([P, PACK, H], F32, name=name)
+            raw = keep.tile([P, PACK, src.shape[1]], F32, name=name)
             nc.sync.dma_start(raw[:], src.rearrange("(p j) c -> p j c", j=PACK))
             return raw
 
         table_bytes = keep.tile([P, T], U8, name="table_bytes", align_bytes=64)
         l_three = load_list("l_three", three)
-        l_offs = load_list("l_offs", offs)
-        l_two = load_list("l_two", two)
         for q in range(4):
             nc.sync.dma_start(
                 table_bytes[32 * q : 32 * (q + 1), :].bitcast(I32),
                 x_scales[0, 4 * q : 4 * q + 4, :].bitcast(I32).unsqueeze(0).broadcast_to([8, 4, T // 4]),
             )
-        raw3 = load_weight("raw3", w3)
+        l_offs = load_list("l_offs", offs)
+        raw3 = [load_weight("raw3_%d" % h, w3[:, H // 2 * h : H // 2 * (h + 1)]) for h in range(2)]
+        l_two = load_list("l_two", two)
         table_words = keep.tile([P, T], U32, name="table_words", align_bytes=64)
         nc.sync.dma_start(table_words[:].bitcast(I32), x_words[0].rearrange("p n t -> p (n t)").bitcast(I32))
+        gb_t = keep.tile([P, PACK], F32, name="gb_t")
+        nc.sync.dma_start(gb_t[:], gb.rearrange("(p t) o -> p (t o)", t=PACK))
         l4 = load_list("l4", n4)
         l5 = load_list("l5", n5)
         l6 = load_list("l6", n6)
-        raw1 = load_weight("raw1", w1)
-        raw2 = load_weight("raw2", w2)
+        raw1 = [load_weight("raw1", w1)]
+        raw2 = [load_weight("raw2", w2)]
+        ga_t = keep.tile([P, PACK], F32, name="ga_t")
+        nc.sync.dma_start(ga_t[:], ga.rearrange("(p t) o -> p (t o)", t=PACK))
         l1 = load_list("l1", n1)
         l2 = load_list("l2", n2)
         l3 = load_list("l3", n3)
         l7 = load_list("l7", n7)
-
-        ga_t = keep.tile([P, PACK], F32, name="ga_t")
-        gb_t = keep.tile([P, PACK], F32, name="gb_t")
-        nc.gpsimd.dma_start(gb_t[:], gb.rearrange("(p t) o -> p (t o)", t=PACK))
-        nc.gpsimd.dma_start(ga_t[:], ga.rearrange("(p t) o -> p (t o)", t=PACK))
-        half_sign = keep.tile([P, PACK], F32, name="half_sign")
-        gah = keep.tile([P, PACK], F32, name="gah")
-        gbh = keep.tile([P, PACK], F32, name="gbh")
-        nc.gpsimd.tensor_scalar(half_sign[:], gb_t[:], 0.0, -0.5, ALU.is_ge, ALU.add)
-        nc.gpsimd.tensor_tensor(gbh[:], gb_t[:], half_sign[:], ALU.mult)
-        nc.gpsimd.tensor_tensor(gah[:], ga_t[:], half_sign[:], ALU.mult)
 
         def pick_bytes(name, lst):
             got = keep.tile([P, S], U8, name=name, align_bytes=64)
@@ -82,12 +75,17 @@ def tile_picked_twkflowbtop2twicp_none_p_kernel(
             nc.vector.tensor_copy(got[:], table_words[:].indirect(lst[:]))
             return got
 
-        def cast_weight(name, raw):
+        def cast_weight(name, raw, eng):
             grouped = keep.tile([P, PACK * H], BF16, name=name, align_bytes=64)
-            nc.scalar.copy(
-                grouped[:].rearrange("p (t m j) -> p m j t", t=PACK, j=PACK),
-                raw[:].rearrange("p j (m t) -> p m j t", t=PACK),
-            )
+            dealt = grouped[:].rearrange("p (t m j) -> p m j t", t=PACK, j=PACK)
+            share = P // len(raw)
+            for h, piece in enumerate(raw):
+                dst = dealt[:, share * h : share * (h + 1)]
+                src = piece[:].rearrange("p j (m t) -> p m j t", t=PACK)
+                if eng == "S":
+                    nc.scalar.copy(dst, src)
+                else:
+                    nc.gpsimd.tensor_scalar(dst, src, 1.0, 0.0, ALU.mult, ALU.add)
             return grouped
 
         def quantize(name, grouped, width):
@@ -120,72 +118,89 @@ def tile_picked_twkflowbtop2twicp_none_p_kernel(
 
         tiles = range(PACK)
         by3 = pick_bytes("by3", l_three)
-        g3 = cast_weight("g3", raw3)
+        g3 = cast_weight("g3", raw3, "S")
         by1 = pick_bytes("by1", l_offs)
         by2 = pick_bytes("by2", l_two)
         q3 = quantize("q3", g3[:], H)
         wd3 = pick_words("wd3", l_three)
         b_ps = [product(t, q3, slice(P * t, P * (t + 1)), (wd3, by3)) for t in tiles]
+        gb_abs = keep.tile([P, PACK], F32, name="gb_abs")
+        nc.vector.scalar_tensor_tensor(gb_abs[:], gb_t[:], -1.0, gb_t[:], ALU.mult, ALU.max)
         b_win = [window("b_win%d" % t) for t in tiles]
         wd1 = pick_words("wd1", l_offs)
         wd2 = pick_words("wd2", l_two)
+        g1 = cast_weight("g1", raw1, "G")
+        g2 = cast_weight("g2", raw2, "G")
+        half_sign = keep.tile([P, PACK], F32, name="half_sign")
+        gah = keep.tile([P, PACK], F32, name="gah")
+        nc.gpsimd.tensor_scalar(half_sign[:], gb_t[:], 0.0, -0.5, ALU.is_ge, ALU.add)
+        nc.gpsimd.tensor_tensor(gah[:], ga_t[:], half_sign[:], ALU.mult)
+        gaf = keep.tile([P, PACK], F32, name="gaf")
+        nc.gpsimd.tensor_tensor(gaf[:], gah[:], gah[:], ALU.add)
 
         z2b = keep.tile([P, PACK, S], BF16, name="z2b", align_bytes=64)
         zb = keep.tile([P, PACK, S], BF16, name="zb", align_bytes=64)
-        B_ENG = ["VVV","SSS","SSS","SSS"]
+        B_ENG = ["SSVV","SSSV","SSSS","SSSS"]
+        Y_ENG = ["SSSSSGG","SSSSSGG","SSSSVGG","SSSSSVV"]
 
-        def b_tile(t):
-            if t in (0,):
-                nc.vector.tensor_scalar(b_win[t][:, 0:S], b_ps[t][:], gbh[:, t : t + 1], None, ALU.mult)
+        def evac(eng, dst, src, scale):
+            if eng == "V":
+                nc.vector.tensor_scalar(dst, src, scale, None, ALU.mult)
             else:
-                nc.scalar.activation(b_win[t][:, 0:S], b_ps[t][:], ACT.Copy, scale=gbh[:, t : t + 1])
+                nc.scalar.activation(dst, src, ACT.Copy, scale=scale)
+
+        def b_fetch(t):
+            evac(B_ENG[t][0], b_win[t][:, 0:S], b_ps[t][:], gb_abs[:, t : t + 1])
             got = [work.tile([P, S], F32, name="bg%d" % i, bufs=4) for i in range(3)]
-            for g, lst, eng in zip(got, (l4, l5, l6), B_ENG[t]):
+            for g, lst, eng in zip(got, (l4, l5, l6), B_ENG[t][1:]):
                 fetch(eng, g[:], b_win[t], lst[:])
+            return got
+
+        def b_combine(t, got):
             hi = work.tile([P, S], F32, name="hi")
             lo = work.tile([P, S], F32, name="lo")
             mid = work.tile([P, S], F32, name="mid")
             nc.vector.tensor_tensor(hi[:], got[0][:], got[1][:], ALU.max)
             nc.vector.tensor_tensor(lo[:], got[0][:], got[1][:], ALU.min)
             nc.vector.tensor_tensor(mid[:], hi[:], got[2][:], ALU.min)
-            nc.vector.tensor_tensor(hi[:], hi[:], got[2][:], ALU.max)
-            nc.vector.tensor_tensor(mid[:], lo[:], mid[:], ALU.max)
-            nc.vector.scalar_tensor_tensor(z2b[:, t, :], hi[:], 2.0, mid[:], ALU.mult, ALU.subtract)
+            nc.vector.tensor_tensor(got[0][:], hi[:], got[2][:], ALU.max)
+            nc.vector.tensor_tensor(got[1][:], lo[:], mid[:], ALU.max)
+            nc.vector.scalar_tensor_tensor(z2b[:, t, :], got[1][:], -0.5, got[0][:], ALU.mult, ALU.add)
 
         y_win = [window("y_win%d" % t) for t in tiles]
         d_win = [window("d_win%d" % t) for t in tiles]
 
         def y_tile(t):
-            nc.scalar.copy(y_win[t][:, 0:S], y_ps[t][:])
+            ey, ed, f1, f2, f3, em, ea = Y_ENG[t]
+            evac(ey, y_win[t][:, 0:S], y_ps[t][:], 1.0)
             y1 = work.tile([P, S], F32, name="y1", bufs=4)
             y2 = work.tile([P, S], F32, name="y2", bufs=4)
-            fetch("S", y2[:], y_win[t], l2[:])
-            nc.scalar.activation(d_win[t][:, 0:S], d_ps[t][:], ACT.Copy, scale=gah[:, t : t + 1])
-            fetch("S", y1[:], y_win[t], l1[:])
             p2 = work.tile([P, S], F32, name="p2", bufs=4)
-            nc.vector.tensor_tensor(y2[:], y2[:], y_win[t][:, 0:S], ALU.subtract)
-            if t in (0, 1):
+            fetch(f1, y1[:], y_win[t], l1[:])
+            evac(ed, d_win[t][:, 0:S], d_ps[t][:], gah[:, t : t + 1])
+            fetch(f2, y2[:], y_win[t], l2[:])
+            if f3 != "F":
+                fetch(f3, p2[:], d_win[t], l3[:])
+            nc.vector.tensor_tensor(y1[:], y1[:], y_ps[t][:], ALU.subtract)
+            nc.vector.tensor_tensor(y2[:], y2[:], y_ps[t][:], ALU.subtract)
+            nc.vector.scalar_tensor_tensor(y1[:], d_ps[t][:], gaf[:, t : t + 1], y1[:], ALU.mult, ALU.mult)
+            if f3 == "F":
                 nc.vector.tensor_tensor(p2[:], d_win[t][:].indirect(l3[:]), y2[:], ALU.mult)
             else:
-                fetch("S", p2[:], d_win[t], l3[:])
-                nc.vector.tensor_tensor(p2[:], p2[:], y2[:], ALU.mult)
-            nc.vector.tensor_tensor(y1[:], y1[:], y_win[t][:, 0:S], ALU.subtract)
-            nc.vector.scalar_tensor_tensor(y1[:], d_win[t][:, 0:S], 2.0, y1[:], ALU.mult, ALU.mult)
-            nc.vector.tensor_tensor(zb[:, t, :], y1[:], p2[:], ALU.add)
+                (nc.gpsimd if em == "G" else nc.vector).tensor_tensor(p2[:], p2[:], y2[:], ALU.mult)
+            (nc.gpsimd if ea == "G" else nc.vector).tensor_tensor(zb[:, t, :], y1[:], p2[:], ALU.add)
 
-        g1 = cast_weight("g1", raw1)
-        g2 = cast_weight("g2", raw2)
-        b_tile(0)
+        gots = [b_fetch(t) for t in tiles]
+        b_combine(0, gots[0])
         q1 = quantize("q1", g1[:], H)
         y_ps = [product(4 + t, q1, slice(P * t, P * (t + 1)), (wd1, by1)) for t in tiles]
+        b_combine(1, gots[1])
         q2 = quantize("q2", g2[:], H)
-        b_tile(1)
-        b_tile(2)
-        b_tile(3)
         d_ps = [product(t, q2, slice(P * t, P * (t + 1)), (wd2, by2)) for t in tiles]
-        for t in tiles:
+        b_combine(2, gots[2])
+        b_combine(3, gots[3])
+        for t in range(4):
             y_tile(t)
-
         z2g = keep.tile([P, PACK * S], BF16, name="z2g", align_bytes=64)
         mov_c = keep.tile([P, S], U32, name="mov_c", align_bytes=64)
         mov_s = keep.tile([P, S], U8, name="mov_s", align_bytes=64)
@@ -200,25 +215,31 @@ def tile_picked_twkflowbtop2twicp_none_p_kernel(
             cols = slice(half * h, half * (h + 1))
             nc.vector.quantize_mx(out=mov_c[:, cols].bitcast(FP8X4), scales=mov_s[:, cols], in_=piece)
 
+        for t in range(4, PACK):
+            y_tile(t)
+
         out_rows = out.rearrange("(g u q) v -> u g q v", u=PACK, q=8)
         s_win = b_win
         st_win = d_win
+        s_ps = []
         for u in tiles:
             zg = keep.tile([P, PACK * P], BF16, name="zg%d" % u, align_bytes=64)
-            nc.vector.tensor_copy(
+            weave = nc.scalar.copy if "VVVV"[u] == "S" else nc.vector.tensor_copy
+            weave(
                 zg[:].rearrange("p (g h i t) -> p g h t i", h=2, i=4, t=PACK),
                 zb[:].rearrange("p t (g u h i) -> p u g h t i", u=PACK, h=2, i=4)[:, u],
             )
             qz = quantize("qz%d" % u, zg[:], P)
-            s_ps = product(4 + u, qz, slice(0, P), (mov_c, mov_s))
-            if u in (0, 1, 2, 3):
-                nc.vector.tensor_scalar(s_win[u][:, 0:S], s_ps[:], 0.0625, None, ALU.mult)
-            else:
-                nc.scalar.mul(s_win[u][:, 0:S], s_ps[:], 0.0625)
+            s_ps.append(product(4 + u, qz, slice(0, P), (mov_c, mov_s)))
+        for u in tiles:
+            evac("VVVV"[u], s_win[u][:, 0:S], s_ps[u][:], 0.0625)
         for u in tiles:
             gate = work.tile([P, S], F32, name="gate", bufs=4)
             nc.scalar.activation(gate[:], s_win[u][:].indirect(l7[:]), ACT.Sigmoid)
-            nc.vector.tensor_tensor(st_win[u][:, 0:S], s_win[u][:, 0:S], gate[:], ALU.mult)
+            if "VVVV"[u] == "G":
+                nc.gpsimd.tensor_tensor(st_win[u][:, 0:S], s_win[u][:, 0:S], gate[:], ALU.mult)
+            else:
+                nc.vector.scalar_tensor_tensor(st_win[u][:, 0:S], s_ps[u][:], 0.0625, gate[:], ALU.mult, ALU.mult)
         for u in tiles:
             other = work.tile([P, S], F32, name="other", bufs=4)
             engs = ["V","S","S","SS"][u]

@@ -53,13 +53,13 @@ def tile_picked_twkflowbtop2twicp_none_p_kernel(
         nc.sync.dma_start(table_words[:].bitcast(I32), x_words[0].rearrange("p n t -> p (n t)").bitcast(I32))
         gb_t = keep.tile([P, PACK], F32, name="gb_t")
         nc.sync.dma_start(gb_t[:], gb.rearrange("(p t) o -> p (t o)", t=PACK))
+        ga_t = keep.tile([P, PACK], F32, name="ga_t")
+        nc.sync.dma_start(ga_t[:], ga.rearrange("(p t) o -> p (t o)", t=PACK))
         l4 = load_list("l4", n4)
         l5 = load_list("l5", n5)
         l6 = load_list("l6", n6)
         raw1 = [load_weight("raw1", w1)]
         raw2 = [load_weight("raw2", w2)]
-        ga_t = keep.tile([P, PACK], F32, name="ga_t")
-        nc.sync.dma_start(ga_t[:], ga.rearrange("(p t) o -> p (t o)", t=PACK))
         l1 = load_list("l1", n1)
         l2 = load_list("l2", n2)
         l3 = load_list("l3", n3)
@@ -75,23 +75,27 @@ def tile_picked_twkflowbtop2twicp_none_p_kernel(
             nc.vector.tensor_copy(got[:], table_words[:].indirect(lst[:]))
             return got
 
-        def cast_weight(name, raw, eng):
+        def cast_weight(name, raw, tile_groups):
             grouped = keep.tile([P, PACK * H], BF16, name=name, align_bytes=64)
             dealt = grouped[:].rearrange("p (t m j) -> p m j t", t=PACK, j=PACK)
             share = P // len(raw)
             for h, piece in enumerate(raw):
-                dst = dealt[:, share * h : share * (h + 1)]
                 src = piece[:].rearrange("p j (m t) -> p m j t", t=PACK)
-                if eng == "S":
-                    nc.scalar.copy(dst, src)
-                else:
-                    nc.gpsimd.tensor_scalar(dst, src, 1.0, 0.0, ALU.mult, ALU.add)
+                for ts in tile_groups:
+                    dst = dealt[:, share * h : share * (h + 1), :, ts]
+                    nc.gpsimd.tensor_scalar(dst, src[:, :, :, ts], 1.0, 0.0, ALU.mult, ALU.add)
             return grouped
 
-        def quantize(name, grouped, width):
+        def quantize(name, grouped, width, parts=1):
             codes = keep.tile([P, width], U32, name=name + "_c", align_bytes=64)
             scales = keep.tile([P, width], U8, name=name + "_s", align_bytes=64)
-            nc.vector.quantize_mx(out=codes[:].bitcast(FP8X4), scales=scales[:], in_=grouped)
+            n = width // parts
+            for k in range(parts):
+                nc.vector.quantize_mx(
+                    out=codes[:, n * k : n * (k + 1)].bitcast(FP8X4),
+                    scales=scales[:, n * k : n * (k + 1)],
+                    in_=grouped[:, PACK * n * k : PACK * n * (k + 1)],
+                )
             return codes, scales
 
         def product(bank, lhs, lhs_cols, rhs):
@@ -118,30 +122,30 @@ def tile_picked_twkflowbtop2twicp_none_p_kernel(
 
         tiles = range(PACK)
         by3 = pick_bytes("by3", l_three)
-        g3 = cast_weight("g3", raw3, "S")
+        g3 = cast_weight("g3", raw3, [slice(0, 2), slice(2, 4)])
         by1 = pick_bytes("by1", l_offs)
         by2 = pick_bytes("by2", l_two)
-        q3 = quantize("q3", g3[:], H)
+        q3 = quantize("q3", g3[:], H, 2)
         wd3 = pick_words("wd3", l_three)
         b_ps = [product(t, q3, slice(P * t, P * (t + 1)), (wd3, by3)) for t in tiles]
         gb_abs = keep.tile([P, PACK], F32, name="gb_abs")
-        nc.vector.scalar_tensor_tensor(gb_abs[:], gb_t[:], -1.0, gb_t[:], ALU.mult, ALU.max)
-        b_win = [window("b_win%d" % t) for t in tiles]
-        wd1 = pick_words("wd1", l_offs)
-        wd2 = pick_words("wd2", l_two)
-        g1 = cast_weight("g1", raw1, "G")
-        g2 = cast_weight("g2", raw2, "G")
         half_sign = keep.tile([P, PACK], F32, name="half_sign")
-        gah = keep.tile([P, PACK], F32, name="gah")
         nc.gpsimd.tensor_scalar(half_sign[:], gb_t[:], 0.0, -0.5, ALU.is_ge, ALU.add)
+        nc.gpsimd.tensor_tensor(gb_abs[:], gb_t[:], half_sign[:], ALU.mult)
+        gah = keep.tile([P, PACK], F32, name="gah")
         nc.gpsimd.tensor_tensor(gah[:], ga_t[:], half_sign[:], ALU.mult)
         gaf = keep.tile([P, PACK], F32, name="gaf")
         nc.gpsimd.tensor_tensor(gaf[:], gah[:], gah[:], ALU.add)
+        b_win = [window("b_win%d" % t) for t in tiles]
+        wd1 = pick_words("wd1", l_offs)
+        wd2 = pick_words("wd2", l_two)
+        g1 = cast_weight("g1", raw1, [slice(0, 4)])
+        g2 = cast_weight("g2", raw2, [slice(0, 4)])
 
         z2b = keep.tile([P, PACK, S], BF16, name="z2b", align_bytes=64)
         zb = keep.tile([P, PACK, S], BF16, name="zb", align_bytes=64)
         B_ENG = ["SSVV","SSSV","SSSS","SSSS"]
-        Y_ENG = ["SSSSSGG","SSSSSGG","SSSSVGG","SSSSSVV"]
+        Y_ENG = ["SSSSSGG","SSSSSGG","SSSSSVV","SSSSSVV"]
 
         def evac(eng, dst, src, scale):
             if eng == "V":
@@ -165,7 +169,7 @@ def tile_picked_twkflowbtop2twicp_none_p_kernel(
             nc.vector.tensor_tensor(mid[:], hi[:], got[2][:], ALU.min)
             nc.vector.tensor_tensor(got[0][:], hi[:], got[2][:], ALU.max)
             nc.vector.tensor_tensor(got[1][:], lo[:], mid[:], ALU.max)
-            nc.vector.scalar_tensor_tensor(z2b[:, t, :], got[1][:], -0.5, got[0][:], ALU.mult, ALU.add)
+            nc.vector.scalar_tensor_tensor(z2b[:, t, :], got[0][:], 2.0, got[1][:], ALU.mult, ALU.subtract)
 
         y_win = [window("y_win%d" % t) for t in tiles]
         d_win = [window("d_win%d" % t) for t in tiles]
@@ -184,10 +188,11 @@ def tile_picked_twkflowbtop2twicp_none_p_kernel(
             nc.vector.tensor_tensor(y1[:], y1[:], y_ps[t][:], ALU.subtract)
             nc.vector.tensor_tensor(y2[:], y2[:], y_ps[t][:], ALU.subtract)
             nc.vector.scalar_tensor_tensor(y1[:], d_ps[t][:], gaf[:, t : t + 1], y1[:], ALU.mult, ALU.mult)
-            if f3 == "F":
-                nc.vector.tensor_tensor(p2[:], d_win[t][:].indirect(l3[:]), y2[:], ALU.mult)
-            else:
-                (nc.gpsimd if em == "G" else nc.vector).tensor_tensor(p2[:], p2[:], y2[:], ALU.mult)
+            return y1, y2, p2
+
+        def y_sum(t, y1, y2, p2):
+            ey, ed, f1, f2, f3, em, ea = Y_ENG[t]
+            (nc.gpsimd if em == "G" else nc.vector).tensor_tensor(p2[:], p2[:], y2[:], ALU.mult)
             (nc.gpsimd if ea == "G" else nc.vector).tensor_tensor(zb[:, t, :], y1[:], p2[:], ALU.add)
 
         gots = [b_fetch(t) for t in tiles]
@@ -199,24 +204,16 @@ def tile_picked_twkflowbtop2twicp_none_p_kernel(
         d_ps = [product(t, q2, slice(P * t, P * (t + 1)), (wd2, by2)) for t in tiles]
         b_combine(2, gots[2])
         b_combine(3, gots[3])
-        for t in range(4):
-            y_tile(t)
         z2g = keep.tile([P, PACK * S], BF16, name="z2g", align_bytes=64)
-        mov_c = keep.tile([P, S], U32, name="mov_c", align_bytes=64)
-        mov_s = keep.tile([P, S], U8, name="mov_s", align_bytes=64)
-        half = S // 2
-        for h in range(2):
-            piece = z2g[:, PACK * half * h : PACK * half * (h + 1)]
-            weave = nc.scalar.copy if "SS"[h] == "S" else nc.vector.tensor_copy
-            weave(
-                piece.rearrange("p (c i t) -> p c t i", t=PACK, i=4),
-                z2b[:, :, half * h : half * (h + 1)].rearrange("p t (c i) -> p c t i", i=4),
-            )
-            cols = slice(half * h, half * (h + 1))
-            nc.vector.quantize_mx(out=mov_c[:, cols].bitcast(FP8X4), scales=mov_s[:, cols], in_=piece)
-
-        for t in range(4, PACK):
-            y_tile(t)
+        nc.vector.tensor_copy(
+            z2g[:].rearrange("p (c i t) -> p c t i", t=PACK, i=4),
+            z2b[:].rearrange("p t (c i) -> p c t i", i=4),
+        )
+        for t in tiles:
+            parts = y_tile(t)
+            if t == 0:
+                mov_c, mov_s = quantize("qmov", z2g[:], S)
+            y_sum(t, *parts)
 
         out_rows = out.rearrange("(g u q) v -> u g q v", u=PACK, q=8)
         s_win = b_win
@@ -233,19 +230,30 @@ def tile_picked_twkflowbtop2twicp_none_p_kernel(
             s_ps.append(product(4 + u, qz, slice(0, P), (mov_c, mov_s)))
         for u in tiles:
             evac("VVVV"[u], s_win[u][:, 0:S], s_ps[u][:], 0.0625)
-        for u in tiles:
+        def pieces(n):
+            return [slice(S // n * k, S // n * (k + 1)) for k in range(n)]
+
+        def offsets(lst, cols):
+            return lst[:, cols.start // 16 : cols.stop // 16]
+
+        def gate_tile(u):
             gate = work.tile([P, S], F32, name="gate", bufs=4)
             nc.scalar.activation(gate[:], s_win[u][:].indirect(l7[:]), ACT.Sigmoid)
             if "VVVV"[u] == "G":
                 nc.gpsimd.tensor_tensor(st_win[u][:, 0:S], s_win[u][:, 0:S], gate[:], ALU.mult)
             else:
                 nc.vector.scalar_tensor_tensor(st_win[u][:, 0:S], s_ps[u][:], 0.0625, gate[:], ALU.mult, ALU.mult)
-        for u in tiles:
+
+        def out_tile(u):
             other = work.tile([P, S], F32, name="other", bufs=4)
-            engs = ["V","S","S","SS"][u]
-            n = S // len(engs)
-            for k, eng in enumerate(engs):
-                cols = slice(n * k, n * (k + 1))
-                fetch(eng, other[:, cols], st_win[u], l7[:, n // 16 * k : n // 16 * (k + 1)])
+            engs = ["V","S","S","VS"][u]
+            for eng, cols in zip(engs, pieces(len(engs))):
+                fetch(eng, other[:, cols], st_win[u], offsets(l7, cols))
                 nc.vector.tensor_tensor(other[:, cols], st_win[u][:, cols], other[:, cols], ALU.max)
                 nc.sync.dma_start(out_rows[u][:, :, cols], other[:, cols])
+
+        gate_tile(0)
+        for u in tiles:
+            if u + 1 < PACK:
+                gate_tile(u + 1)
+            out_tile(u)

@@ -129,6 +129,8 @@ def tile_picked_twkflowbtop2twicp_none_p_kernel(
         wd3 = pick_words("wd3", l_three)
         b_ps = [product(t, q3, slice(P * t, P * (t + 1)), (wd3, by3)) for t in tiles]
         gb_abs = keep.tile([P, PACK], F32, name="gb_abs")
+        warm = keep.tile([P, 1], F32, name="warm")
+        nc.scalar.activation(warm[:], gb_t[:, 0:1], ACT.Sigmoid)
         half_sign = keep.tile([P, PACK], F32, name="half_sign")
         nc.gpsimd.tensor_scalar(half_sign[:], gb_t[:], 0.0, -0.5, ALU.is_ge, ALU.add)
         nc.gpsimd.tensor_tensor(gb_abs[:], gb_t[:], half_sign[:], ALU.mult)

from contextlib import ExitStack

import concourse.mybir as mybir

K, T, S, H = 512, 2048, 512, 512
FLOPS = 4 * 2 * 512 * 512 * 512

F32 = mybir.dt.float32
BF16 = mybir.dt.bfloat16
I32 = mybir.dt.int32
U32 = mybir.dt.uint32
U16 = mybir.dt.uint16
U8 = mybir.dt.uint8
FP8X4 = mybir.dt.float8_e4m3fn_x4
ALU = mybir.AluOpType
ACT = mybir.ActivationFunctionType

P = 128
PACK = 4
WIN = 2 * S


def tile_picked_twkflowbtop2twicp_none_p_kernel(
    tc, x_words, x_scales, w1, w2, w3, ga, gb, offs, two, n1, n2, n3, three, n4, n5, n6, n7, out
):
    nc = tc.nc
    with ExitStack() as ctx:
        keep = ctx.enter_context(tc.tile_pool(name="keep", bufs=1))
        work = ctx.enter_context(tc.tile_pool(name="work", bufs=2))
        psum = ctx.enter_context(tc.psum_pool(name="psum", bufs=1))

        def load_list(name, src):
            tile = keep.tile([P, S // 16], U16, name=name)
            nc.sync.dma_start(tile[:], src)
            return tile

        def load_weight(name, src):
            raw = keep.tile([P, PACK, src.shape[1]], F32, name=name)
            nc.sync.dma_start(raw[:], src.rearrange("(p j) c -> p j c", j=PACK))
            return raw

        table_bytes = keep.tile([P, T], U8, name="table_bytes", align_bytes=64)
        l_three = load_list("l_three", three)
        for q in range(4):
            nc.sync.dma_start(
                table_bytes[32 * q : 32 * (q + 1), :].bitcast(I32),
                x_scales[0, 4 * q : 4 * q + 4, :].bitcast(I32).unsqueeze(0).broadcast_to([8, 4, T // 4]),
            )
        l_offs = load_list("l_offs", offs)
        raw3 = [load_weight("raw3_%d" % h, w3[:, H // 2 * h : H // 2 * (h + 1)]) for h in range(2)]
        l_two = load_list("l_two", two)
        table_words = keep.tile([P, T], U32, name="table_words", align_bytes=64)
        nc.sync.dma_start(table_words[:].bitcast(I32), x_words[0].rearrange("p n t -> p (n t)").bitcast(I32))
        gb_t = keep.tile([P, PACK], F32, name="gb_t")
        nc.sync.dma_start(gb_t[:], gb.rearrange("(p t) o -> p (t o)", t=PACK))
        ga_t = keep.tile([P, PACK], F32, name="ga_t")
        nc.sync.dma_start(ga_t[:], ga.rearrange("(p t) o -> p (t o)", t=PACK))
        l4 = load_list("l4", n4)
        l5 = load_list("l5", n5)
        l6 = load_list("l6", n6)
        raw1 = [load_weight("raw1", w1)]
        raw2 = [load_weight("raw2", w2)]
        l1 = load_list("l1", n1)
        l2 = load_list("l2", n2)
        l3 = load_list("l3", n3)
        l7 = load_list("l7", n7)

        def pick_bytes(name, lst):
            got = keep.tile([P, S], U8, name=name, align_bytes=64)
            nc.vector.tensor_copy(got[:], table_bytes[:].indirect(lst[:]))
            return got

        def pick_words(name, lst):
            got = keep.tile([P, S], U32, name=name, align_bytes=64)
            nc.vector.tensor_copy(got[:], table_words[:].indirect(lst[:]))
            return got

        def cast_weight(name, raw, tile_groups):
            grouped = keep.tile([P, PACK * H], BF16, name=name, align_bytes=64)
            dealt = grouped[:].rearrange("p (t m j) -> p m j t", t=PACK, j=PACK)
            share = P // len(raw)
            for h, piece in enumerate(raw):
                src = piece[:].rearrange("p j (m t) -> p m j t", t=PACK)
                for ts in tile_groups:
                    dst = dealt[:, share * h : share * (h + 1), :, ts]
                    nc.gpsimd.tensor_scalar(dst, src[:, :, :, ts], 1.0, 0.0, ALU.mult, ALU.add)
            return grouped

        def quantize(name, grouped, width, parts=1):
            codes = keep.tile([P, width], U32, name=name + "_c", align_bytes=64)
            scales = keep.tile([P, width], U8, name=name + "_s", align_bytes=64)
            n = width // parts
            for k in range(parts):
                nc.vector.quantize_mx(
                    out=codes[:, n * k : n * (k + 1)].bitcast(FP8X4),
                    scales=scales[:, n * k : n * (k + 1)],
                    in_=grouped[:, PACK * n * k : PACK * n * (k + 1)],
                )
            return codes, scales

        def product(bank, lhs, lhs_cols, rhs):
            acc = psum.tile([P, S], F32, name="bank%d" % bank)
            nc.tensor.matmul_mx(
                out=acc[:],
                lhsT=lhs[0][:, lhs_cols].bitcast(FP8X4),
                lhsT_scale=lhs[1][:, lhs_cols],
                rhs=rhs[0][:].bitcast(FP8X4),
                rhs_scale=rhs[1][:],
                start=True,
                stop=True,
            )
            return acc

        def window(name):
            return keep.tile([P, WIN], F32, name=name)

        def fetch(engine, dst, win, lst):
            if engine == "S":
                nc.scalar.activation(dst, win[:].indirect(lst), ACT.Copy)
            else:
                nc.vector.tensor_copy(dst, win[:].indirect(lst))

        tiles = range(PACK)
        by3 = pick_bytes("by3", l_three)
        g3 = cast_weight("g3", raw3, [slice(0, 2), slice(2, 4)])
        by1 = pick_bytes("by1", l_offs)
        by2 = pick_bytes("by2", l_two)
        q3 = quantize("q3", g3[:], H, 2)
        wd3 = pick_words("wd3", l_three)
        b_ps = [product(t, q3, slice(P * t, P * (t + 1)), (wd3, by3)) for t in tiles]
        gb_abs = keep.tile([P, PACK], F32, name="gb_abs")
        warm = keep.tile([P, 1], F32, name="warm")
        nc.scalar.activation(warm[:], gb_t[:, 0:1], ACT.Sigmoid)
        half_sign = keep.tile([P, PACK], F32, name="half_sign")
        nc.gpsimd.tensor_scalar(half_sign[:], gb_t[:], 0.0, -0.5, ALU.is_ge, ALU.add)
        nc.gpsimd.tensor_tensor(gb_abs[:], gb_t[:], half_sign[:], ALU.mult)
        gah = keep.tile([P, PACK], F32, name="gah")
        nc.gpsimd.tensor_tensor(gah[:], ga_t[:], half_sign[:], ALU.mult)
        gaf = keep.tile([P, PACK], F32, name="gaf")
        nc.gpsimd.tensor_tensor(gaf[:], gah[:], gah[:], ALU.add)
        b_win = [window("b_win%d" % t) for t in tiles]
        wd1 = pick_words("wd1", l_offs)
        wd2 = pick_words("wd2", l_two)
        g1 = cast_weight("g1", raw1, [slice(0, 4)])
        g2 = cast_weight("g2", raw2, [slice(0, 4)])

        z2b = keep.tile([P, PACK, S], BF16, name="z2b", align_bytes=64)
        zb = keep.tile([P, PACK, S], BF16, name="zb", align_bytes=64)
        B_ENG = ["SSVV","SSSV","SSSS","SSSS"]
        Y_ENG = ["SSSSSGG","SSSSSGG","SSSSSVV","SSSSSVV"]

        def evac(eng, dst, src, scale):
            if eng == "V":
                nc.vector.tensor_scalar(dst, src, scale, None, ALU.mult)
            else:
                nc.scalar.activation(dst, src, ACT.Copy, scale=scale)

        def b_fetch(t):
            evac(B_ENG[t][0], b_win[t][:, 0:S], b_ps[t][:], gb_abs[:, t : t + 1])
            got = [work.tile([P, S], F32, name="bg%d" % i, bufs=4) for i in range(3)]
            for g, lst, eng in zip(got, (l4, l5, l6), B_ENG[t][1:]):
                fetch(eng, g[:], b_win[t], lst[:])
            return got

        def b_combine(t, got):
            hi = work.tile([P, S], F32, name="hi")
            lo = work.tile([P, S], F32, name="lo")
            mid = work.tile([P, S], F32, name="mid")
            nc.vector.tensor_tensor(hi[:], got[0][:], got[1][:], ALU.max)
            nc.vector.tensor_tensor(lo[:], got[0][:], got[1][:], ALU.min)
            nc.vector.tensor_tensor(mid[:], hi[:], got[2][:], ALU.min)
            nc.vector.tensor_tensor(got[0][:], hi[:], got[2][:], ALU.max)
            nc.vector.tensor_tensor(got[1][:], lo[:], mid[:], ALU.max)
            nc.vector.scalar_tensor_tensor(z2b[:, t, :], got[0][:], 2.0, got[1][:], ALU.mult, ALU.subtract)

        y_win = [window("y_win%d" % t) for t in tiles]
        d_win = [window("d_win%d" % t) for t in tiles]

        def y_tile(t):
            ey, ed, f1, f2, f3, em, ea = Y_ENG[t]
            evac(ey, y_win[t][:, 0:S], y_ps[t][:], 1.0)
            y1 = work.tile([P, S], F32, name="y1", bufs=4)
            y2 = work.tile([P, S], F32, name="y2", bufs=4)
            p2 = work.tile([P, S], F32, name="p2", bufs=4)
            fetch(f1, y1[:], y_win[t], l1[:])
            evac(ed, d_win[t][:, 0:S], d_ps[t][:], gah[:, t : t + 1])
            fetch(f2, y2[:], y_win[t], l2[:])
            if f3 != "F":
                fetch(f3, p2[:], d_win[t], l3[:])
            nc.vector.tensor_tensor(y1[:], y1[:], y_ps[t][:], ALU.subtract)
            nc.vector.tensor_tensor(y2[:], y2[:], y_ps[t][:], ALU.subtract)
            nc.vector.scalar_tensor_tensor(y1[:], d_ps[t][:], gaf[:, t : t + 1], y1[:], ALU.mult, ALU.mult)
            return y1, y2, p2

        def y_sum(t, y1, y2, p2):
            ey, ed, f1, f2, f3, em, ea = Y_ENG[t]
            (nc.gpsimd if em == "G" else nc.vector).tensor_tensor(p2[:], p2[:], y2[:], ALU.mult)
            (nc.gpsimd if ea == "G" else nc.vector).tensor_tensor(zb[:, t, :], y1[:], p2[:], ALU.add)

        gots = [b_fetch(t) for t in tiles]
        b_combine(0, gots[0])
        q1 = quantize("q1", g1[:], H)
        y_ps = [product(4 + t, q1, slice(P * t, P * (t + 1)), (wd1, by1)) for t in tiles]
        b_combine(1, gots[1])
        q2 = quantize("q2", g2[:], H)
        d_ps = [product(t, q2, slice(P * t, P * (t + 1)), (wd2, by2)) for t in tiles]
        b_combine(2, gots[2])
        b_combine(3, gots[3])
        z2g = keep.tile([P, PACK * S], BF16, name="z2g", align_bytes=64)
        nc.vector.tensor_copy(
            z2g[:].rearrange("p (c i t) -> p c t i", t=PACK, i=4),
            z2b[:].rearrange("p t (c i) -> p c t i", i=4),
        )
        for t in tiles:
            parts = y_tile(t)
            if t == 0:
                mov_c, mov_s = quantize("qmov", z2g[:], S)
            y_sum(t, *parts)

        out_rows = out.rearrange("(g u q) v -> u g q v", u=PACK, q=8)
        s_win = b_win
        st_win = d_win
        s_ps = []
        for u in tiles:
            zg = keep.tile([P, PACK * P], BF16, name="zg%d" % u, align_bytes=64)
            weave = nc.scalar.copy if "VVVV"[u] == "S" else nc.vector.tensor_copy
            weave(
                zg[:].rearrange("p (g h i t) -> p g h t i", h=2, i=4, t=PACK),
                zb[:].rearrange("p t (g u h i) -> p u g h t i", u=PACK, h=2, i=4)[:, u],
            )
            qz = quantize("qz%d" % u, zg[:], P)
            s_ps.append(product(4 + u, qz, slice(0, P), (mov_c, mov_s)))
        for u in tiles:
            evac("VVVV"[u], s_win[u][:, 0:S], s_ps[u][:], 0.0625)
        def pieces(n):
            return [slice(S // n * k, S // n * (k + 1)) for k in range(n)]

        def offsets(lst, cols):
            return lst[:, cols.start // 16 : cols.stop // 16]

        def gate_tile(u):
            gate = work.tile([P, S], F32, name="gate", bufs=4)
            nc.scalar.activation(gate[:], s_win[u][:].indirect(l7[:]), ACT.Sigmoid)
            if "VVVV"[u] == "G":
                nc.gpsimd.tensor_tensor(st_win[u][:, 0:S], s_win[u][:, 0:S], gate[:], ALU.mult)
            else:
                nc.vector.scalar_tensor_tensor(st_win[u][:, 0:S], s_ps[u][:], 0.0625, gate[:], ALU.mult, ALU.mult)

        def out_tile(u):
            other = work.tile([P, S], F32, name="other", bufs=4)
            engs = ["V","S","S","VS"][u]
            for eng, cols in zip(engs, pieces(len(engs))):
                fetch(eng, other[:, cols], st_win[u], offsets(l7, cols))
                nc.vector.tensor_tensor(other[:, cols], st_win[u][:, cols], other[:, cols], ALU.max)
                nc.sync.dma_start(out_rows[u][:, :, cols], other[:, cols])

        gate_tile(0)
        for u in tiles:
            if u + 1 < PACK:
                gate_tile(u + 1)
            out_tile(u)
